import numpy as np
import ml_dtypes

BF16 = ml_dtypes.bfloat16


def bf(x):
    return np.asarray(x, np.float32).astype(BF16)


def f32(x):
    return np.asarray(x, np.float32)


def f64(x):
    return np.asarray(x).astype(np.float64)


def striped(idx):
    return np.concatenate([l.reshape(-1, 16).T for l in idx])


def rows(idx, k):
    return np.tile(np.repeat(idx, 16, axis=0), (k // (16 * 8), 1))


def look(tab, idx):
    return np.take_along_axis(f64(tab), rows(idx, len(tab)), axis=1)


K, S, D, V, N, M = 256, 2048, 3, 512, 1536, 256


def setup_inputs():
    return {"tab": bf(0.7 * np.random.standard_normal((D, K, S))), "base": bf(np.random.standard_normal((K, V))), "w": bf(np.random.standard_normal((K, M)) / np.sqrt(K)), "offs": striped(np.random.randint(0, S, (8, N)))}


def reference(tab, base, w, offs):
    idx = np.stack([g.T.reshape(-1) for g in np.split(offs, 8)])
    x = f64(base) + sum(look(tab[d], idx[:, d * V:(d + 1) * V]) for d in range(D))
    y = f64(w).T @ x
    return y

@@ -1,0 +1,70 @@
+import concourse.mybir as mybir
+
+STAGES, ROWS, CODEWORDS, VECTORS, OUTPUTS = 3, 256, 2048, 512, 256
+PARTITIONS = 128
+BLOCKS = ROWS // PARTITIONS
+OUT_BLOCKS = OUTPUTS // PARTITIONS
+ENTRIES_PER_COLUMN = 16
+PIECE = VECTORS // ENTRIES_PER_COLUMN
+
+FLOPS = 2 * ROWS * OUTPUTS * VECTORS + STAGES * ROWS * VECTORS
+
+BF16, F32, U16 = mybir.dt.bfloat16, mybir.dt.float32, mybir.dt.uint16
+ADD = mybir.AluOpType.add
+
+
+def tile_lookup_res_add_none_kernel(tc, tab, base, w, offs, out):
+    nc = tc.nc
+    with (
+        tc.tile_pool(name="held", bufs=1) as held,
+        tc.psum_pool(name="psum", bufs=1) as psum,
+    ):
+        offsets = held.tile([PARTITIONS, STAGES * PIECE], U16, name="offsets")
+        nc.sync.dma_start(offsets[:], offs)
+        base_bf16 = held.tile([PARTITIONS, BLOCKS, VECTORS], BF16, name="base_bf16")
+        nc.sync.dma_start(base_bf16[:], base.rearrange("(b p) v -> p b v", p=PARTITIONS))
+
+        stages_and_blocks = [(d, b) for d in range(STAGES) for b in range(BLOCKS)]
+        loaded = {}
+        for d, b in stages_and_blocks:
+            codebook = held.tile([PARTITIONS, CODEWORDS], BF16, name=f"codebook_{d}_{b}")
+            nc.sync.dma_start(codebook[:], tab[d, b * PARTITIONS : (b + 1) * PARTITIONS, :])
+            loaded[d, b] = codebook
+        weights = held.tile([PARTITIONS, BLOCKS, OUTPUTS], BF16, name="weights")
+        nc.sync.dma_start(weights[:], w.rearrange("(b p) m -> p b m", p=PARTITIONS))
+
+        base_f32 = held.tile([PARTITIONS, BLOCKS, VECTORS], F32, name="base_f32")
+        nc.vector.tensor_copy(base_f32[:], base_bf16[:])
+        sums = [base_f32[:, b, :] for b in range(BLOCKS)]
+
+        for d, b in stages_and_blocks:
+            window = held.tile([PARTITIONS, CODEWORDS], F32, name=f"window_{d}_{b}")
+            if b == 0:
+                nc.vector.tensor_copy(window[:], loaded[d, b][:])
+            else:
+                nc.scalar.copy(window[:], loaded[d, b][:])
+            picked = window[:].indirect(offsets[:, d * PIECE : (d + 1) * PIECE])
+            total = held.tile([PARTITIONS, VECTORS], F32, name=f"total_{d}_{b}")
+            nc.vector.tensor_tensor(total[:], picked, sums[b], ADD)
+            sums[b] = total[:]
+
+        products = [psum.tile([PARTITIONS, VECTORS], F32, name=f"product_{m}") for m in range(OUT_BLOCKS)]
+        for b in range(BLOCKS):
+            x = held.tile([PARTITIONS, VECTORS], BF16, name=f"x_{b}")
+            nc.vector.tensor_copy(x[:], sums[b])
+            for m in range(OUT_BLOCKS):
+                nc.tensor.matmul(
+                    products[m][:],
+                    weights[:, b, m * PARTITIONS : (m + 1) * PARTITIONS],
+                    x[:],
+                    start=b == 0,
+                    stop=b == BLOCKS - 1,
+                )
+
+        for m in range(OUT_BLOCKS):
+            result = held.tile([PARTITIONS, VECTORS], F32, name=f"result_{m}")
+            if m == 0:
+                nc.scalar.copy(result[:], products[m][:])
+            else:
+                nc.vector.tensor_copy(result[:], products[m][:])
+            nc.sync.dma_start(out[m * PARTITIONS : (m + 1) * PARTITIONS, :], result[:])

@@ -10,40 +10,58 @@ PIECE = VECTORS // ENTRIES_PER_COLUMN
 FLOPS = 2 * ROWS * OUTPUTS * VECTORS + STAGES * ROWS * VECTORS
 
 BF16, F32, U16 = mybir.dt.bfloat16, mybir.dt.float32, mybir.dt.uint16
+VECTOR_PART = 3
+ALIGNED = 16
+
 ADD = mybir.AluOpType.add
 
 
 def tile_lookup_res_add_none_kernel(tc, tab, base, w, offs, out):
     nc = tc.nc
+
+    def cast(wide, narrow, width):
+        cut = width // VECTOR_PART // ALIGNED * ALIGNED
+        nc.vector.tensor_copy(wide[:, :cut], narrow[:, :cut])
+        nc.scalar.copy(wide[:, cut:], narrow[:, cut:])
+
     with (
         tc.tile_pool(name="held", bufs=1) as held,
         tc.psum_pool(name="psum", bufs=1) as psum,
     ):
-        offsets = held.tile([PARTITIONS, STAGES * PIECE], U16, name="offsets")
-        nc.sync.dma_start(offsets[:], offs)
-        base_bf16 = held.tile([PARTITIONS, BLOCKS, VECTORS], BF16, name="base_bf16")
-        nc.sync.dma_start(base_bf16[:], base.rearrange("(b p) v -> p b v", p=PARTITIONS))
-
         stages_and_blocks = [(d, b) for d in range(STAGES) for b in range(BLOCKS)]
-        loaded = {}
+        codebooks = {}
         for d, b in stages_and_blocks:
             codebook = held.tile([PARTITIONS, CODEWORDS], BF16, name=f"codebook_{d}_{b}")
             nc.sync.dma_start(codebook[:], tab[d, b * PARTITIONS : (b + 1) * PARTITIONS, :])
-            loaded[d, b] = codebook
+            codebooks[d, b] = codebook
+            if (d, b) == (0, 0):
+                offsets = held.tile([PARTITIONS, STAGES * PIECE], U16, name="offsets")
+                nc.sync.dma_start(offsets[:], offs)
+                base_bf16 = held.tile([PARTITIONS, BLOCKS * VECTORS], BF16, name="base_bf16")
+                nc.sync.dma_start(
+                    base_bf16[:].rearrange("p (b v) -> p b v", b=BLOCKS),
+                    base.rearrange("(b p) v -> p b v", p=PARTITIONS),
+                )
         weights = held.tile([PARTITIONS, BLOCKS, OUTPUTS], BF16, name="weights")
         nc.sync.dma_start(weights[:], w.rearrange("(b p) m -> p b m", p=PARTITIONS))
 
-        base_f32 = held.tile([PARTITIONS, BLOCKS, VECTORS], F32, name="base_f32")
-        nc.vector.tensor_copy(base_f32[:], base_bf16[:])
-        sums = [base_f32[:, b, :] for b in range(BLOCKS)]
+        windows = {}
 
-        for d, b in stages_and_blocks:
+        def make_window(d, b):
             window = held.tile([PARTITIONS, CODEWORDS], F32, name=f"window_{d}_{b}")
-            if b == 0:
-                nc.vector.tensor_copy(window[:], loaded[d, b][:])
-            else:
-                nc.scalar.copy(window[:], loaded[d, b][:])
-            picked = window[:].indirect(offsets[:, d * PIECE : (d + 1) * PIECE])
+            cast(window, codebooks[d, b], CODEWORDS)
+            windows[d, b] = window
+
+        make_window(0, 0)
+
+        base_f32 = held.tile([PARTITIONS, BLOCKS * VECTORS], F32, name="base_f32")
+        cast(base_f32, base_bf16, BLOCKS * VECTORS)
+        sums = [base_f32[:, b * VECTORS : (b + 1) * VECTORS] for b in range(BLOCKS)]
+
+        for step, (d, b) in enumerate(stages_and_blocks):
+            if step + 1 < len(stages_and_blocks):
+                make_window(*stages_and_blocks[step + 1])
+            picked = windows[d, b][:].indirect(offsets[:, d * PIECE : (d + 1) * PIECE])
             total = held.tile([PARTITIONS, VECTORS], F32, name=f"total_{d}_{b}")
             nc.vector.tensor_tensor(total[:], picked, sums[b], ADD)
             sums[b] = total[:]

@@ -13,14 +13,21 @@ BF16, F32, U16 = mybir.dt.bfloat16, mybir.dt.float32, mybir.dt.uint16
 VECTOR_PART = 3
 ALIGNED = 16
 
+ALIGNED = 16
+HALVES = 2
+HALF = VECTORS // HALVES
+
 ADD = mybir.AluOpType.add
 
 
 def tile_lookup_res_add_none_kernel(tc, tab, base, w, offs, out):
     nc = tc.nc
 
-    def cast(wide, narrow, width):
-        cut = width // VECTOR_PART // ALIGNED * ALIGNED
+    def rows(block):
+        return slice(block * PARTITIONS, (block + 1) * PARTITIONS)
+
+    def cast(wide, narrow, width, vector_thirds):
+        cut = vector_thirds * width // 3 // ALIGNED * ALIGNED
         nc.vector.tensor_copy(wide[:, :cut], narrow[:, :cut])
         nc.scalar.copy(wide[:, cut:], narrow[:, cut:])
 
@@ -28,61 +35,69 @@ def tile_lookup_res_add_none_kernel(tc, tab, base, w, offs, out):
         tc.tile_pool(name="held", bufs=1) as held,
         tc.psum_pool(name="psum", bufs=1) as psum,
     ):
+        offsets = held.tile([PARTITIONS, STAGES * PIECE], U16, name="offsets")
+        nc.sync.dma_start(offsets[:], offs)
+
         stages_and_blocks = [(d, b) for d in range(STAGES) for b in range(BLOCKS)]
+        bases = []
         codebooks = {}
         for d, b in stages_and_blocks:
+            if d == 0:
+                base_bf16 = held.tile([PARTITIONS, VECTORS], BF16, name=f"base_bf16_{b}")
+                nc.sync.dma_start(base_bf16[:], base[rows(b), :])
+                bases.append(base_bf16)
             codebook = held.tile([PARTITIONS, CODEWORDS], BF16, name=f"codebook_{d}_{b}")
-            nc.sync.dma_start(codebook[:], tab[d, b * PARTITIONS : (b + 1) * PARTITIONS, :])
+            nc.sync.dma_start(codebook[:], tab[d, rows(b), :])
             codebooks[d, b] = codebook
-            if (d, b) == (0, 0):
-                offsets = held.tile([PARTITIONS, STAGES * PIECE], U16, name="offsets")
-                nc.sync.dma_start(offsets[:], offs)
-                base_bf16 = held.tile([PARTITIONS, BLOCKS * VECTORS], BF16, name="base_bf16")
-                nc.sync.dma_start(
-                    base_bf16[:].rearrange("p (b v) -> p b v", b=BLOCKS),
-                    base.rearrange("(b p) v -> p b v", p=PARTITIONS),
-                )
         weights = held.tile([PARTITIONS, BLOCKS, OUTPUTS], BF16, name="weights")
         nc.sync.dma_start(weights[:], w.rearrange("(b p) m -> p b m", p=PARTITIONS))
 
+        sums = []
         windows = {}
 
-        def make_window(d, b):
+        def prepare(d, b):
+            vector_thirds = 2 if (d, b) == (0, 0) else 1
+            if d == 0:
+                start = held.tile([PARTITIONS, VECTORS], F32, name=f"start_{b}")
+                cast(start, bases[b], VECTORS, vector_thirds)
+                sums.append(start)
             window = held.tile([PARTITIONS, CODEWORDS], F32, name=f"window_{d}_{b}")
-            cast(window, codebooks[d, b], CODEWORDS)
+            cast(window, codebooks[d, b], CODEWORDS, vector_thirds)
             windows[d, b] = window
 
-        make_window(0, 0)
-
-        base_f32 = held.tile([PARTITIONS, BLOCKS * VECTORS], F32, name="base_f32")
-        cast(base_f32, base_bf16, BLOCKS * VECTORS)
-        sums = [base_f32[:, b * VECTORS : (b + 1) * VECTORS] for b in range(BLOCKS)]
-
+        prepare(0, 0)
         for step, (d, b) in enumerate(stages_and_blocks):
             if step + 1 < len(stages_and_blocks):
-                make_window(*stages_and_blocks[step + 1])
+                prepare(*stages_and_blocks[step + 1])
             picked = windows[d, b][:].indirect(offsets[:, d * PIECE : (d + 1) * PIECE])
             total = held.tile([PARTITIONS, VECTORS], F32, name=f"total_{d}_{b}")
-            nc.vector.tensor_tensor(total[:], picked, sums[b], ADD)
-            sums[b] = total[:]
+            nc.vector.tensor_tensor(total[:], picked, sums[b][:], ADD)
+            sums[b] = total
 
-        products = [psum.tile([PARTITIONS, VECTORS], F32, name=f"product_{m}") for m in range(OUT_BLOCKS)]
+        x = [held.tile([PARTITIONS, VECTORS], BF16, name=f"x_{b}") for b in range(BLOCKS)]
+        products = {
+            (m, h): psum.tile([PARTITIONS, HALF], F32, name=f"product_{m}_{h}")
+            for m in range(OUT_BLOCKS)
+            for h in range(HALVES)
+        }
         for b in range(BLOCKS):
-            x = held.tile([PARTITIONS, VECTORS], BF16, name=f"x_{b}")
-            nc.vector.tensor_copy(x[:], sums[b])
-            for m in range(OUT_BLOCKS):
-                nc.tensor.matmul(
-                    products[m][:],
-                    weights[:, b, m * PARTITIONS : (m + 1) * PARTITIONS],
-                    x[:],
-                    start=b == 0,
-                    stop=b == BLOCKS - 1,
-                )
+            nc.vector.tensor_copy(x[b][:, :HALF], sums[b][:, :HALF])
+            nc.scalar.copy(x[b][:, HALF:], sums[b][:, HALF:])
+            for h in range(HALVES):
+                for m in range(OUT_BLOCKS):
+                    nc.tensor.matmul(
+                        products[m, h][:],
+                        weights[:, b, rows(m)],
+                        x[b][:, h * HALF : (h + 1) * HALF],
+                        start=b == 0,
+                        stop=b == BLOCKS - 1,
+                    )
 
-        for m in range(OUT_BLOCKS):
-            result = held.tile([PARTITIONS, VECTORS], F32, name=f"result_{m}")
-            if m == 0:
-                nc.scalar.copy(result[:], products[m][:])
-            else:
-                nc.vector.tensor_copy(result[:], products[m][:])
-            nc.sync.dma_start(out[m * PARTITIONS : (m + 1) * PARTITIONS, :], result[:])
+        for h in range(HALVES):
+            for m in range(OUT_BLOCKS):
+                result = held.tile([PARTITIONS, HALF], F32, name=f"result_{m}_{h}")
+                if m == 0:
+                    nc.scalar.copy(result[:], products[m, h][:])
+                else:
+                    nc.vector.tensor_copy(result[:], products[m, h][:])
+                nc.sync.dma_start(out[rows(m), h * HALF : (h + 1) * HALF], result[:])

@@ -16,6 +16,7 @@ ALIGNED = 16
 ALIGNED = 16
 HALVES = 2
 HALF = VECTORS // HALVES
+WARM_UPS = 6
 
 ADD = mybir.AluOpType.add
 
@@ -65,24 +66,29 @@ def tile_lookup_res_add_none_kernel(tc, tab, base, w, offs, out):
             cast(window, codebooks[d, b], CODEWORDS, vector_thirds)
             windows[d, b] = window
 
-        prepare(0, 0)
-        for step, (d, b) in enumerate(stages_and_blocks):
-            if step + 1 < len(stages_and_blocks):
-                prepare(*stages_and_blocks[step + 1])
-            picked = windows[d, b][:].indirect(offsets[:, d * PIECE : (d + 1) * PIECE])
-            total = held.tile([PARTITIONS, VECTORS], F32, name=f"total_{d}_{b}")
-            nc.vector.tensor_tensor(total[:], picked, sums[b][:], ADD)
-            sums[b] = total
-
         x = [held.tile([PARTITIONS, VECTORS], BF16, name=f"x_{b}") for b in range(BLOCKS)]
         products = {
             (m, h): psum.tile([PARTITIONS, HALF], F32, name=f"product_{m}_{h}")
             for m in range(OUT_BLOCKS)
             for h in range(HALVES)
         }
-        for b in range(BLOCKS):
-            nc.vector.tensor_copy(x[b][:, :HALF], sums[b][:, :HALF])
-            nc.scalar.copy(x[b][:, HALF:], sums[b][:, HALF:])
+
+        warm_up = psum.tile([PARTITIONS, VECTORS], F32, name="warm_up")
+        for repeat in range(WARM_UPS):
+            nc.tensor.matmul(
+                warm_up[:],
+                weights[:, 0, rows(0)],
+                codebooks[STAGES - 1, BLOCKS - 1][:, :VECTORS],
+                start=True,
+                stop=True,
+            )
+
+        def project(b):
+            if b < BLOCKS - 1:
+                nc.scalar.copy(x[b][:], sums[b][:])
+            else:
+                nc.vector.tensor_copy(x[b][:, :HALF], sums[b][:, :HALF])
+                nc.scalar.copy(x[b][:, HALF:], sums[b][:, HALF:])
             for h in range(HALVES):
                 for m in range(OUT_BLOCKS):
                     nc.tensor.matmul(
@@ -92,6 +98,17 @@ def tile_lookup_res_add_none_kernel(tc, tab, base, w, offs, out):
                         start=b == 0,
                         stop=b == BLOCKS - 1,
                     )
+
+        prepare(0, 0)
+        for step, (d, b) in enumerate(stages_and_blocks):
+            if step + 1 < len(stages_and_blocks):
+                prepare(*stages_and_blocks[step + 1])
+            picked = windows[d, b][:].indirect(offsets[:, d * PIECE : (d + 1) * PIECE])
+            total = held.tile([PARTITIONS, VECTORS], F32, name=f"total_{d}_{b}")
+            nc.vector.tensor_tensor(total[:], picked, sums[b][:], ADD)
+            sums[b] = total
+            if d == STAGES - 1:
+                project(b)
 
         for h in range(HALVES):
             for m in range(OUT_BLOCKS):

import concourse.mybir as mybir

STAGES, ROWS, CODEWORDS, VECTORS, OUTPUTS = 3, 256, 2048, 512, 256
PARTITIONS = 128
BLOCKS = ROWS // PARTITIONS
OUT_BLOCKS = OUTPUTS // PARTITIONS
ENTRIES_PER_COLUMN = 16
PIECE = VECTORS // ENTRIES_PER_COLUMN

FLOPS = 2 * ROWS * OUTPUTS * VECTORS + STAGES * ROWS * VECTORS

BF16, F32, U16 = mybir.dt.bfloat16, mybir.dt.float32, mybir.dt.uint16
VECTOR_PART = 3
ALIGNED = 16

ALIGNED = 16
HALVES = 2
HALF = VECTORS // HALVES
WARM_UPS = 6

ADD = mybir.AluOpType.add


def tile_lookup_res_add_none_kernel(tc, tab, base, w, offs, out):
    nc = tc.nc

    def rows(block):
        return slice(block * PARTITIONS, (block + 1) * PARTITIONS)

    def cast(wide, narrow, width, vector_thirds):
        cut = vector_thirds * width // 3 // ALIGNED * ALIGNED
        nc.vector.tensor_copy(wide[:, :cut], narrow[:, :cut])
        nc.scalar.copy(wide[:, cut:], narrow[:, cut:])

    with (
        tc.tile_pool(name="held", bufs=1) as held,
        tc.psum_pool(name="psum", bufs=1) as psum,
    ):
        offsets = held.tile([PARTITIONS, STAGES * PIECE], U16, name="offsets")
        nc.sync.dma_start(offsets[:], offs)

        stages_and_blocks = [(d, b) for d in range(STAGES) for b in range(BLOCKS)]
        bases = []
        codebooks = {}
        for d, b in stages_and_blocks:
            if d == 0:
                base_bf16 = held.tile([PARTITIONS, VECTORS], BF16, name=f"base_bf16_{b}")
                nc.sync.dma_start(base_bf16[:], base[rows(b), :])
                bases.append(base_bf16)
            codebook = held.tile([PARTITIONS, CODEWORDS], BF16, name=f"codebook_{d}_{b}")
            nc.sync.dma_start(codebook[:], tab[d, rows(b), :])
            codebooks[d, b] = codebook
        weights = held.tile([PARTITIONS, BLOCKS, OUTPUTS], BF16, name="weights")
        nc.sync.dma_start(weights[:], w.rearrange("(b p) m -> p b m", p=PARTITIONS))

        sums = []
        windows = {}

        def prepare(d, b):
            vector_thirds = 2 if (d, b) == (0, 0) else 1
            if d == 0:
                start = held.tile([PARTITIONS, VECTORS], F32, name=f"start_{b}")
                cast(start, bases[b], VECTORS, vector_thirds)
                sums.append(start)
            window = held.tile([PARTITIONS, CODEWORDS], F32, name=f"window_{d}_{b}")
            cast(window, codebooks[d, b], CODEWORDS, vector_thirds)
            windows[d, b] = window

        x = [held.tile([PARTITIONS, VECTORS], BF16, name=f"x_{b}") for b in range(BLOCKS)]
        products = {
            (m, h): psum.tile([PARTITIONS, HALF], F32, name=f"product_{m}_{h}")
            for m in range(OUT_BLOCKS)
            for h in range(HALVES)
        }

        warm_up = psum.tile([PARTITIONS, VECTORS], F32, name="warm_up")
        for repeat in range(WARM_UPS):
            nc.tensor.matmul(
                warm_up[:],
                weights[:, 0, rows(0)],
                codebooks[STAGES - 1, BLOCKS - 1][:, :VECTORS],
                start=True,
                stop=True,
            )

        def project(b):
            if b < BLOCKS - 1:
                nc.scalar.copy(x[b][:], sums[b][:])
            else:
                nc.vector.tensor_copy(x[b][:, :HALF], sums[b][:, :HALF])
                nc.scalar.copy(x[b][:, HALF:], sums[b][:, HALF:])
            for h in range(HALVES):
                for m in range(OUT_BLOCKS):
                    nc.tensor.matmul(
                        products[m, h][:],
                        weights[:, b, rows(m)],
                        x[b][:, h * HALF : (h + 1) * HALF],
                        start=b == 0,
                        stop=b == BLOCKS - 1,
                    )

        prepare(0, 0)
        for step, (d, b) in enumerate(stages_and_blocks):
            if step + 1 < len(stages_and_blocks):
                prepare(*stages_and_blocks[step + 1])
            picked = windows[d, b][:].indirect(offsets[:, d * PIECE : (d + 1) * PIECE])
            total = held.tile([PARTITIONS, VECTORS], F32, name=f"total_{d}_{b}")
            nc.vector.tensor_tensor(total[:], picked, sums[b][:], ADD)
            sums[b] = total
            if d == STAGES - 1:
                project(b)

        for h in range(HALVES):
            for m in range(OUT_BLOCKS):
                result = held.tile([PARTITIONS, HALF], F32, name=f"result_{m}_{h}")
                if m == 0:
                    nc.scalar.copy(result[:], products[m, h][:])
                else:
                    nc.vector.tensor_copy(result[:], products[m, h][:])
                nc.sync.dma_start(out[rows(m), h * HALF : (h + 1) * HALF], result[:])
